import numpy as np, ml_dtypes
CORES = [56,61,80,85]
N = 4
import mx_ref
NC, G, KO, SH = 128, 2, 1, 3
C = np.float32(0.047)
BF = ml_dtypes.bfloat16
def cut(t, i, w=512):
    return t[:, w * i:w * i + w]
def tile(rs):
    return np.stack(rs, axis=2).reshape(128, -1).astype(BF)
def layer(w, X):
    out = []
    for i in range(G):
        for t in range(len(X)):
            p = mx_ref.matmul(mx_ref.quantize(cut(w, len(X) * i + t)), X[t])
            z = p if t == 0 else z + p
        out.append(z)
    return out
def act(Z):
    return [np.maximum(s * z, 0) * C for z in Z for s in (1, -1)]
def inputs(rng, e, E):
    def f(*shape):
        v = (rng.standard_normal(shape, dtype=np.float32) * np.exp2(rng.integers(-2, 3, shape[:-1] + (1,)))).astype(BF)
        return mx_ref.spread((v.astype(np.float32) * np.exp2(rng.integers(-E, E + 1, shape[:-2] + (1, 1))).astype(np.float32)).astype(BF), rng, e)
    def packed(k):
        c = np.zeros((N, 128, k * 512), np.uint8); s = np.zeros((N, 128, k * 128), np.uint8)
        for r in range(N):
            for i in range(k):
                a, b = mx_ref.quantize(f(128, 512)); c[r][:, 512 * i:512 * i + 512] = a; s[r][:, 128 * i:128 * i + 128] = mx_ref.plane(b, rng)
        return c, s
    d = {}
    d["kc"], d["ks"] = packed(KO)
    d["x"] = f(N, 128, 4 * NC)
    d["wk"] = f(N, 128, G * 512)
    d["q"] = f(N, 128, 512)
    return d
def setup_inputs(rng):
    return inputs(rng, 0, 0)
def setup_inputs_blocks(rng):
    return inputs(rng, 4, 0)
def setup_inputs_wide(rng):
    return inputs(rng, 0, 8)
def reference(kc, ks, x, wk, q):
    new = [mx_ref.quantize(tile(act(layer(wk[r], [mx_ref.quantize(x[r])])))) for r in range(N)]
    y = np.zeros((N, 128, 128 * KO + NC), np.float32)
    for o in range(N):
        old = (np.ascontiguousarray(kc[o]), mx_ref.live(ks[o]))
        qq = mx_ref.quantize(q[o])
        y[o] = np.concatenate([mx_ref.matmul(qq, old), mx_ref.matmul(qq, new[(o - SH) % N])], axis=1)
    return {"y": y}

import numpy as np
from concourse.mybir import dt, AluOpType, ActivationFunctionType

SCRATCH = {
    "xb": ("sbuf", [128, 512], "bfloat16"),
    "wb": ("sbuf", [128, 1024], "bfloat16"),
    "qb": ("sbuf", [128, 512], "bfloat16"),
    "h": ("sbuf", [128, 512], "bfloat16"),
    "cx": ("sbuf", [128, 128], "float8_e4m3fn_x4"), "sx": ("sbuf", [128, 128], "uint8"),
    "cw0": ("sbuf", [128, 128], "float8_e4m3fn_x4"), "sw0": ("sbuf", [128, 128], "uint8"),
    "cw1": ("sbuf", [128, 128], "float8_e4m3fn_x4"), "sw1": ("sbuf", [128, 128], "uint8"),
    "cq": ("sbuf", [128, 128], "float8_e4m3fn_x4"), "sq": ("sbuf", [128, 128], "uint8"),
    "ck": ("sbuf", [128, 128], "float8_e4m3fn_x4"), "sk": ("sbuf", [128, 128], "uint8"),
    "co": ("sbuf", [128, 128], "float8_e4m3fn_x4"), "so": ("sbuf", [128, 128], "uint8"),
    "ca": ("sbuf", [128, 128], "float8_e4m3fn_x4"), "sa": ("sbuf", [128, 128], "uint8"),
    "z0": ("psum", [128, 512], "float32"),
    "z1": ("psum", [128, 512], "float32"),
    "po": ("psum", [128, 512], "float32"),
    "pn": ("psum", [128, 512], "float32"),
    "yo": ("sbuf", [128, 128], "float32"),
    "yn": ("sbuf", [128, 128], "float32"),
}
SEMAPHORES = ["l_x", "l_w0", "l_w1", "l_q", "l_k", "q_x", "q_w0", "q_w1", "q_q", "q_k", "m_z0", "m_z1", "m_o", "m_n",
              "a_s", "a_v", "e_o", "e_n", "st", "arr_c", "arr_s", "sent"]

SHIFT = 3
SCALE = float(np.float32(0.047))
SIM_CORES = 96
ENG_CODES = 8
ENG_PLANE = 8


def _mask(topo, src, dst, n):
    full = topo.mask(src, dst)
    bits = [b for b in range(full.bit_length()) if (full >> b) & 1]
    n = min(n, len(bits))
    step = len(bits) // n
    return sum(1 << b for b in bits[::step][:n]), n


def _ways(T, topo):
    n = len(T.cores)
    used = set(T.cores)
    ways = []
    for r in range(n):
        src, dst = T.cores[r], T.cores[(r + SHIFT) % n]
        if topo.may_write(src, dst):
            ways.append(([src, dst], [src, dst]))
            continue
        able = [c for c in range(SIM_CORES)
                if topo.chip(c) == topo.chip(src) and c not in used and topo.may_write(c, dst)]
        near = [c for c in able if topo.die(c) == topo.die(src)]
        far = [c for c in able if topo.die(c) != topo.die(src)]
        used.update((near[0], far[0]))
        ways.append(([src, near[0], dst], [src, far[0], dst]))
    return ways


def _send(g, T, topo, src, dst, plane, codes_buf, plane_buf):
    mask, n = _mask(topo, src, dst, ENG_PLANE if plane else ENG_CODES)
    rid, pid, _ = topo.addr(dst)
    if plane:
        g.remote_dma(T.sa[:, 0:128], plane_buf[:, 0:128], T.sem.arr_s, T.sem.sent, pid, rid, mask)
    else:
        g.remote_dma(T.ca[:, 0:128].bitcast(dt.uint8), codes_buf[:, 0:128].bitcast(dt.uint8),
                     T.sem.arr_c, T.sem.sent, pid, rid, mask)
    return n


def _came(topo, way, at, plane):
    return _mask(topo, way[at - 1], way[at], ENG_PLANE if plane else ENG_CODES)[1]


def rank_program(g, core, T, topo):
    ways = _ways(T, topo)
    rank = T.rank_of(core)
    if rank is None:
        for pair in ways:
            for plane, way in ((False, pair[0]), (True, pair[1])):
                if core in way[1:-1]:
                    at = way.index(core)
                    g.wait_ge(T.sem.arr_s if plane else T.sem.arr_c, _came(topo, way, at, plane))
                    n = _send(g, T, topo, core, way[at + 1], plane, T.ca, T.sa)
                    g.wait_ge(T.sem.sent, n)
        return
    s = T.sem
    n_ranks = len(T.cores)
    give = ways[rank]
    take = ways[(rank - SHIFT) % n_ranks]
    mult, vmax = AluOpType.mult, AluOpType.max
    relu = ActivationFunctionType.Relu

    g.sync.dma_start(T.xb[:, 0:512], T.x[:, 0:512]).then_inc(s.l_x, 16)
    g.sync.dma_start(T.wb[:, 512:1024], T.wk[:, 512:1024]).then_inc(s.l_w1, 16)
    g.sync.wait_ge(s.l_w1, 16)
    g.sync.dma_start(T.qb[:, 0:512], T.q[:, 0:512]).then_inc(s.l_q, 16)
    g.sync.dma_start(T.co[:, 0:128].bitcast(dt.uint8), T.kc[:, 0:512]).then_inc(s.l_k, 16)
    g.sync.dma_start(T.so[:, 0:128], T.ks[:, 0:128]).then_inc(s.l_k, 16)
    g.sync.wait_ge(s.e_o, 1)
    g.sync.dma_start(T.y[:, 0:128], T.yo[:, 0:128]).then_inc(s.st, 16)
    g.sync.wait_ge(s.e_n, 1)
    g.sync.dma_start(T.y[:, 128:256], T.yn[:, 0:128]).then_inc(s.st, 16)
    g.sync.wait_ge(s.st, 32)

    g.scalar.dma_start(T.wb[:, 0:512], T.wk[:, 0:512]).then_inc(s.l_w0, 16)
    g.scalar.wait_ge(s.m_z0, 1)
    g.scalar.activation(T.h[:, 0:512:4], T.z0[:, 0:128], relu, scale=SCALE).then_inc(s.a_s, 1)
    g.scalar.activation(T.h[:, 1:512:4], T.z0[:, 0:128], relu, scale=-SCALE).then_inc(s.a_s, 1)

    g.vector.wait_ge(s.l_x, 16)
    g.vector.quantize_mx(T.cx[:, 0:128], T.sx[:, 0:128], T.xb[:, 0:512]).then_inc(s.q_x, 1)
    g.vector.wait_ge(s.l_w0, 16)
    g.vector.quantize_mx(T.cw0[:, 0:128], T.sw0[:, 0:128], T.wb[:, 0:512]).then_inc(s.q_w0, 1)
    g.vector.wait_ge(s.l_w1, 16)
    g.vector.quantize_mx(T.cw1[:, 0:128], T.sw1[:, 0:128], T.wb[:, 512:1024]).then_inc(s.q_w1, 1)
    g.vector.wait_ge(s.m_z1, 1)
    g.vector.tensor_scalar(T.h[:, 2:512:4], T.z1[:, 0:128], SCALE, 0.0, mult, vmax).then_inc(s.a_v, 1)
    g.vector.tensor_scalar(T.h[:, 3:512:4], T.z1[:, 0:128], -SCALE, 0.0, mult, vmax).then_inc(s.a_v, 1)
    g.vector.wait_ge(s.a_s, 2)
    g.vector.wait_ge(s.a_v, 2)
    g.vector.quantize_mx(T.ck[:, 0:128], T.sk[:, 0:128], T.h[:, 0:512]).then_inc(s.q_k, 1)
    g.vector.wait_ge(s.l_q, 16)
    g.vector.quantize_mx(T.cq[:, 0:128], T.sq[:, 0:128], T.qb[:, 0:512]).then_inc(s.q_q, 1)
    g.vector.wait_ge(s.m_o, 1)
    g.vector.tensor_copy(T.yo[:, 0:128], T.po[:, 0:128]).then_inc(s.e_o, 1)
    g.vector.wait_ge(s.m_n, 1)
    g.vector.tensor_copy(T.yn[:, 0:128], T.pn[:, 0:128]).then_inc(s.e_n, 1)

    g.tensor.wait_ge(s.q_x, 1)
    g.tensor.wait_ge(s.q_w0, 1)
    g.tensor.matmul_mx(T.z0[:, 0:128], T.cw0[:, 0:128], T.sw0[:, 0:128], T.cx[:, 0:128], T.sx[:, 0:128],
                       True, True).then_inc(s.m_z0, 1)
    g.tensor.wait_ge(s.q_w1, 1)
    g.tensor.matmul_mx(T.z1[:, 0:128], T.cw1[:, 0:128], T.sw1[:, 0:128], T.cx[:, 0:128], T.sx[:, 0:128],
                       True, True).then_inc(s.m_z1, 1)
    g.tensor.wait_ge(s.l_k, 32)
    g.tensor.wait_ge(s.q_q, 1)
    g.tensor.matmul_mx(T.po[:, 0:128], T.cq[:, 0:128], T.sq[:, 0:128], T.co[:, 0:128], T.so[:, 0:128],
                       True, True).then_inc(s.m_o, 1)
    g.tensor.wait_ge(s.arr_s, _came(topo, take[1], len(take[1]) - 1, True))
    g.tensor.wait_ge(s.arr_c, _came(topo, take[0], len(take[0]) - 1, False))
    g.tensor.matmul_mx(T.pn[:, 0:128], T.cq[:, 0:128], T.sq[:, 0:128], T.ca[:, 0:128], T.sa[:, 0:128],
                       True, True).then_inc(s.m_n, 1)

    g.wait_ge(s.q_k, 1)
    n = _send(g, T, topo, core, give[0][1], False, T.ck, T.sk)
    n += _send(g, T, topo, core, give[1][1], True, T.ck, T.sk)
    g.wait_ge(s.sent, n)
